import numpy as np
import ml_dtypes


def mxq(x, axis, fmt="e4m3"):
    dtype, down = {"e4m3": (ml_dtypes.float8_e4m3fn, 7), "e5m2": (ml_dtypes.float8_e5m2, 14)}[fmt]
    v = np.moveaxis(np.asarray(x, np.float32).astype(ml_dtypes.bfloat16).astype(np.float64), axis, -1)
    blocks = v.reshape(v.shape[:-1] + (-1, 32))
    amax = np.abs(blocks).max(-1, keepdims=True)
    byte = np.maximum(np.where(amax > 0, np.frexp(amax)[1] - 1 + 127, 0) - down, 1)
    scale = np.exp2(byte - 127.0)
    codes = (blocks / scale).astype(np.float32).astype(dtype).astype(np.float64)
    return np.moveaxis((codes * scale).reshape(v.shape), -1, axis)


WIDE = False


def mx_kscale(k):
    if not WIDE:
        return np.ones(k)
    levels = np.array([10, -10, 5, -5, 0])
    if k % 512:
        return np.exp2(np.random.permutation(np.resize(levels, k // 32))).repeat(32)
    a = np.empty((k // 512, 16))
    for p in range(k // 512):
        a[p, :8] = np.random.permutation(np.resize(levels, 8))
        for g in range(8):
            far = levels[np.abs(levels - a[p, g]) >= 10]
            a[p, g + 8] = far[np.random.randint(len(far))]
    return np.exp2(a.ravel()).repeat(32)


def f64(x):
    return np.asarray(x).astype(np.float64)


def striped(idx):
    return np.tile(np.asarray(idx).reshape(-1, 16).T, (8, 1)).astype(np.uint16)


def unstriped(offs):
    return offs[:16].T.reshape(-1).astype(np.int64)


D, I, T, Q, E = 1024, 512, 512, 128, 512


def setup_inputs():
    n = np.random.standard_normal
    idx = np.random.permutation(D)[:I]
    fi = mx_kscale(I)
    ft = mx_kscale(T)
    ti = np.ones(D)
    ti[idx] = fi
    return {
        "query": (n((Q, D)) * 0.6 / np.sqrt(I) * ti).astype(np.float32),
        "keys": (n((T, D)) / ti).astype(np.float32),
        "size": (np.random.uniform(0.5, 2.0, (1, T)) * ft).astype(np.float32),
        "vals": (n((T, E)) / ft[:, None]).astype(np.float32),
        "offs": striped(idx),
    }


def reference(query, keys, size, vals, offs):
    idx = unstriped(offs)
    qp = f64(query)[:, idx].T
    kp = f64(keys)[:, idx].T
    qpq = mxq(qp, 0, "e4m3")
    kpq = mxq(kp, 0, "e4m3")
    a = qpq.T @ kpq
    p = np.exp(a - np.max(a, axis=1, keepdims=True))
    w = p * f64(size) / np.sum(p, axis=1, keepdims=True)
    wt = w.T
    wtq = mxq(wt, 0, "e4m3")
    valsq = mxq(f64(vals), 0, "e4m3")
    o = wtq.T @ valsq
    return o

@@ -1,0 +1,176 @@
+from contextlib import ExitStack
+
+import concourse.mybir as mybir
+from concourse.masks import make_identity
+
+D, I, T, Q, E = 1024, 512, 512, 128, 512
+FLOPS = 2 * Q * T * I + 2 * Q * E * T
+
+F32 = mybir.dt.float32
+BF16 = mybir.dt.bfloat16
+U32 = mybir.dt.uint32
+U16 = mybir.dt.uint16
+U8 = mybir.dt.uint8
+FP8X4 = mybir.dt.float8_e4m3fn_x4
+ALU = mybir.AluOpType
+ACT = mybir.ActivationFunctionType
+
+P = 128
+PACK = 4
+KEY_TILES = T // P
+HALF = E // 2
+
+
+def tile_attend_sparq_kernel(tc, query, keys, size, vals, offs, out):
+    nc = tc.nc
+    with ExitStack() as ctx:
+        held = ctx.enter_context(tc.tile_pool(name="held", bufs=1))
+        turn = ctx.enter_context(tc.psum_pool(name="turn", bufs=3))
+        banks = ctx.enter_context(tc.psum_pool(name="banks", bufs=1))
+
+        def sbuf(shape, dtype, name, after=None):
+            return held.tile(shape, dtype, name=name, tag=after or name, align_bytes=64)
+
+        offsets = held.tile([P, I // 16], U16, name="offsets")
+        nc.sync.dma_start(offsets[:], offs)
+        q_raw = sbuf([P, D], F32, "q_raw")
+        nc.sync.dma_start(q_raw[:], query)
+        k_raw = []
+        for c in range(KEY_TILES):
+            u, h = divmod(c, 2)
+            raw = sbuf([P, D], F32, f"k_raw{c}")
+            nc.sync.dma_start(raw[:], keys[256 * h + u : 256 * (h + 1) : 2, :])
+            k_raw.append(raw)
+        size_cols = sbuf([P, 2, 2], F32, "size_cols")
+        nc.scalar.dma_start(size_cols[:], size[0, :].rearrange("(h r u) -> r h u", h=2, u=2))
+        v_raw = []
+        for half in range(2):
+            raw = sbuf([P, PACK, HALF], F32, f"v_raw{half}")
+            nc.sync.dma_start(raw[:], vals[:, half * HALF : (half + 1) * HALF].rearrange("(p j) e -> p j e", j=PACK))
+            v_raw.append(raw)
+
+        ident = sbuf([P, P], F32, "ident")
+        make_identity(nc, ident[:])
+        warm = sbuf([P, 1], F32, "warm")
+        nc.scalar.activation(warm[:], ident[:, 0:1], ACT.Exp)
+
+        def quantize(codes, scales, grouped):
+            nc.vector.quantize_mx(out=codes.bitcast(FP8X4), scales=scales, in_=grouped)
+
+        def multiply(dest, lhs_codes, lhs_scales, rhs_codes, rhs_scales):
+            nc.tensor.matmul_mx(
+                out=dest,
+                lhsT=lhs_codes.bitcast(FP8X4),
+                lhsT_scale=lhs_scales,
+                rhs=rhs_codes.bitcast(FP8X4),
+                rhs_scale=rhs_scales,
+                start=True,
+                stop=True,
+            )
+
+        def leave_psum(grouped, turned):
+            nc.scalar.copy(
+                grouped.bitcast(F32).rearrange("p (r u) -> p r u", u=2),
+                turned[:].rearrange("p u r -> p r u"),
+            )
+
+        def gather_and_turn(raw, grouped, name):
+            picked = sbuf([P, I], BF16, f"{name}_picked")
+            nc.vector.tensor_copy(picked[:], raw[:].indirect(offsets[:]))
+            words = picked[:].bitcast(F32)
+            turned = turn.tile([P, 2, P], F32, name="turned")
+            for u in range(2):
+                nc.tensor.transpose(turned[:, u, :], words[:, u : I // 2 : 2], ident[:])
+            leave_psum(grouped, turned)
+            return picked
+
+        size_rows = banks.tile([P, T], F32, name="size_rows")
+        for c in range(KEY_TILES):
+            u, h = divmod(c, 2)
+            nc.tensor.transpose(size_rows[:, c * P : (c + 1) * P], size_cols[:, h, u : u + 1].to_broadcast([P, P]), ident[:])
+
+        first_grouped = sbuf([P, 2 * I], BF16, "first_grouped")
+        mid_grouped = sbuf([P, 2 * I], BF16, "mid_grouped")
+        last_grouped = sbuf([P, I], BF16, "last_grouped")
+        gather_and_turn(q_raw, first_grouped[:, :I], "q")
+        gather_and_turn(k_raw[0], first_grouped[:, I:], "k0")
+        gather_and_turn(k_raw[1], mid_grouped[:, :I], "k1")
+        gather_and_turn(k_raw[2], mid_grouped[:, I:], "k2")
+        last_picked = gather_and_turn(k_raw[3], last_grouped[:], "k3")
+
+
+        first_codes = sbuf([P, 2 * P], U32, "first_codes", after="k_raw3")
+        first_scales = sbuf([P, 2 * P], U8, "first_scales")
+        mid_codes = sbuf([P, 2 * P], U32, "mid_codes")
+        mid_scales = sbuf([P, 2 * P], U8, "mid_scales")
+        last_codes = sbuf([P, P], U32, "last_codes")
+        last_scales = sbuf([P, P], U8, "last_scales")
+        quantize(first_codes[:], first_scales[:], first_grouped[:])
+        quantize(mid_codes[:], mid_scales[:], mid_grouped[:])
+        quantize(last_codes[:], last_scales[:], last_grouped[:])
+
+        q_codes, q_scales = first_codes[:, :P], first_scales[:, :P]
+        first_scores = banks.tile([P, P], F32, name="first_scores")
+        mid_scores = banks.tile([P, 2 * P], F32, name="mid_scores")
+        last_scores = banks.tile([P, P], F32, name="last_scores")
+        multiply(first_scores[:], q_codes, q_scales, first_codes[:, P:], first_scales[:, P:])
+        multiply(mid_scores[:], q_codes, q_scales, mid_codes[:], mid_scales[:])
+        multiply(last_scores[:], q_codes, q_scales, last_codes[:], last_scales[:])
+
+        negated = sbuf([P, T], F32, "negated")
+        first_least = sbuf([P, 1], F32, "first_least")
+        mid_least = sbuf([P, 1], F32, "mid_least")
+        least = sbuf([P, 1], F32, "least")
+        nc.vector.tensor_scalar(negated[:, :P], first_scores[:], -1.0, None, ALU.mult, ALU.min, accum_out=first_least[:])
+        nc.vector.tensor_scalar(negated[:, P : 3 * P], mid_scores[:], -1.0, first_least[:], ALU.mult, ALU.min, accum_out=mid_least[:])
+        nc.vector.tensor_scalar(negated[:, 3 * P :], last_scores[:], -1.0, mid_least[:], ALU.mult, ALU.min, accum_out=least[:])
+
+
+        def interleave(engine_copy, raw, cols, name, after):
+            width = cols.stop - cols.start
+            grouped = sbuf([P, width * PACK], BF16, name, after=after)
+            engine_copy(
+                grouped[:].rearrange("p (c u e) -> p c u e", u=2, e=2),
+                raw[:, :, cols].rearrange("p (e u) c -> p c u e", u=2),
+            )
+            return grouped
+
+        v_grouped0 = interleave(nc.scalar.copy, v_raw[0], slice(0, P), "v_grouped0", "k3_picked")
+
+        p = sbuf([P, T], F32, "p")
+        p_sum = sbuf([P, 1], F32, "p_sum")
+        nc.scalar.activation(p[:], negated[:], ACT.Exp, bias=least[:], scale=-1.0, accum_out=p_sum[:])
+        v_grouped1 = interleave(nc.scalar.copy, v_raw[0], slice(P, HALF), "v_grouped1", "negated")
+        v_grouped2 = interleave(nc.vector.tensor_copy, v_raw[1], slice(0, HALF), "v_grouped2", "mid_least")
+        p_inv = sbuf([P, 1], F32, "p_inv")
+        nc.vector.reciprocal(p_inv[:], p_sum[:])
+
+        w_turned = turn.tile([P, 2, P], F32, name="turned")
+        for u in range(2):
+            cols = slice(u * (T // 2), (u + 1) * (T // 2))
+            w = sbuf([P, T // 2], BF16, f"w{u}")
+            nc.vector.scalar_tensor_tensor(w[:], p[:, cols], p_inv[:], size_rows[:, cols], ALU.mult, ALU.mult)
+            nc.tensor.transpose(w_turned[:, u, :], w[:].bitcast(F32), ident[:])
+        w_grouped = sbuf([P, T], BF16, "w_grouped")
+        leave_psum(w_grouped[:], w_turned)
+
+        v_codes = sbuf([P, E], U32, "v_codes", after="p")
+        v_scales = sbuf([P, E], U8, "v_scales")
+        quantize(v_codes[:, :P], v_scales[:, :P], v_grouped0[:])
+        quantize(v_codes[:, HALF:], v_scales[:, HALF:], v_grouped2[:])
+        quantize(v_codes[:, P:HALF], v_scales[:, P:HALF], v_grouped1[:])
+
+        w_codes = sbuf([P, P], U32, "w_codes")
+        w_scales = sbuf([P, P], U8, "w_scales")
+        quantize(w_codes[:], w_scales[:], w_grouped[:])
+        for half in range(2):
+            cols = slice(half * HALF, (half + 1) * HALF)
+            acc = banks.tile([P, HALF], F32, name=f"acc{half}", tag=("first_scores", "mid_scores")[half])
+            multiply(acc[:], w_codes[:], w_scales[:], v_codes[:, cols], v_scales[:, cols])
+            result = sbuf([P, HALF], F32, f"result{half}")
+            if half == 0:
+                nc.scalar.copy(result[:], acc[:])
+                nc.scalar.dma_start(out[:, cols], result[:])
+            else:
+                nc.vector.tensor_copy(result[:], acc[:])
+                nc.sync.dma_start(out[:, cols], result[:])

@@ -32,17 +32,18 @@ def tile_attend_sparq_kernel(tc, query, keys, size, vals, offs, out):
             return held.tile(shape, dtype, name=name, tag=after or name, align_bytes=64)
 
         offsets = held.tile([P, I // 16], U16, name="offsets")
-        nc.sync.dma_start(offsets[:], offs)
         q_raw = sbuf([P, D], F32, "q_raw")
         nc.sync.dma_start(q_raw[:], query)
+        nc.sync.dma_start(offsets[:], offs)
         k_raw = []
         for c in range(KEY_TILES):
             u, h = divmod(c, 2)
             raw = sbuf([P, D], F32, f"k_raw{c}")
             nc.sync.dma_start(raw[:], keys[256 * h + u : 256 * (h + 1) : 2, :])
             k_raw.append(raw)
-        size_cols = sbuf([P, 2, 2], F32, "size_cols")
-        nc.scalar.dma_start(size_cols[:], size[0, :].rearrange("(h r u) -> r h u", h=2, u=2))
+            if c == 0:
+                size_cols = sbuf([P, 2, 2], F32, "size_cols")
+                nc.sync.dma_start(size_cols[:], size[0, :].rearrange("(h r u) -> r h u", h=2, u=2))
         v_raw = []
         for half in range(2):
             raw = sbuf([P, PACK, HALF], F32, f"v_raw{half}")
@@ -74,13 +75,16 @@ def tile_attend_sparq_kernel(tc, query, keys, size, vals, offs, out):
                 turned[:].rearrange("p u r -> p r u"),
             )
 
-        def gather_and_turn(raw, grouped, name):
+        def scalar_gather(dest, listed):
+            nc.scalar.activation(dest, listed, ACT.Copy)
+
+        def gather_and_turn(gather, raw, grouped, name):
             picked = sbuf([P, I], BF16, f"{name}_picked")
-            nc.vector.tensor_copy(picked[:], raw[:].indirect(offsets[:]))
+            gather(picked[:].rearrange("r (u g y) -> r g u y", u=2, y=16), raw[:].indirect(offsets[:]))
             words = picked[:].bitcast(F32)
             turned = turn.tile([P, 2, P], F32, name="turned")
             for u in range(2):
-                nc.tensor.transpose(turned[:, u, :], words[:, u : I // 2 : 2], ident[:])
+                nc.tensor.transpose(turned[:, u, :], words[:, u * P : (u + 1) * P], ident[:])
             leave_psum(grouped, turned)
             return picked
 
@@ -92,29 +96,31 @@ def tile_attend_sparq_kernel(tc, query, keys, size, vals, offs, out):
         first_grouped = sbuf([P, 2 * I], BF16, "first_grouped")
         mid_grouped = sbuf([P, 2 * I], BF16, "mid_grouped")
         last_grouped = sbuf([P, I], BF16, "last_grouped")
-        gather_and_turn(q_raw, first_grouped[:, :I], "q")
-        gather_and_turn(k_raw[0], first_grouped[:, I:], "k0")
-        gather_and_turn(k_raw[1], mid_grouped[:, :I], "k1")
-        gather_and_turn(k_raw[2], mid_grouped[:, I:], "k2")
-        last_picked = gather_and_turn(k_raw[3], last_grouped[:], "k3")
+        gather_and_turn(nc.vector.tensor_copy, q_raw, first_grouped[:, :I], "q")
+        k0_rounded = sbuf([P, D], BF16, "k0_rounded")
+        nc.vector.tensor_copy(k0_rounded[:], k_raw[0][:])
+        gather_and_turn(scalar_gather, k0_rounded, first_grouped[:, I:], "k0")
+        gather_and_turn(nc.vector.tensor_copy, k_raw[1], mid_grouped[:, :I], "k1")
+        gather_and_turn(nc.vector.tensor_copy, k_raw[2], mid_grouped[:, I:], "k2")
+        last_picked = gather_and_turn(nc.vector.tensor_copy, k_raw[3], last_grouped[:], "k3")
 
-
-        first_codes = sbuf([P, 2 * P], U32, "first_codes", after="k_raw3")
+        early_codes = sbuf([P, 4 * P], U32, "early_codes", after="k_raw3")
+        first_codes, mid_codes = early_codes[:, : 2 * P], early_codes[:, 2 * P :]
         first_scales = sbuf([P, 2 * P], U8, "first_scales")
-        mid_codes = sbuf([P, 2 * P], U32, "mid_codes")
         mid_scales = sbuf([P, 2 * P], U8, "mid_scales")
         last_codes = sbuf([P, P], U32, "last_codes")
         last_scales = sbuf([P, P], U8, "last_scales")
-        quantize(first_codes[:], first_scales[:], first_grouped[:])
-        quantize(mid_codes[:], mid_scales[:], mid_grouped[:])
+        quantize(first_codes, first_scales[:], first_grouped[:])
+        quantize(mid_codes, mid_scales[:], mid_grouped[:])
         quantize(last_codes[:], last_scales[:], last_grouped[:])
+
 
         q_codes, q_scales = first_codes[:, :P], first_scales[:, :P]
         first_scores = banks.tile([P, P], F32, name="first_scores")
         mid_scores = banks.tile([P, 2 * P], F32, name="mid_scores")
         last_scores = banks.tile([P, P], F32, name="last_scores")
         multiply(first_scores[:], q_codes, q_scales, first_codes[:, P:], first_scales[:, P:])
-        multiply(mid_scores[:], q_codes, q_scales, mid_codes[:], mid_scales[:])
+        multiply(mid_scores[:], q_codes, q_scales, mid_codes, mid_scales[:])
         multiply(last_scores[:], q_codes, q_scales, last_codes[:], last_scales[:])
 
         negated = sbuf([P, T], F32, "negated")
@@ -163,14 +169,15 @@ def tile_attend_sparq_kernel(tc, query, keys, size, vals, offs, out):
         w_codes = sbuf([P, P], U32, "w_codes")
         w_scales = sbuf([P, P], U8, "w_scales")
         quantize(w_codes[:], w_scales[:], w_grouped[:])
-        for half in range(2):
-            cols = slice(half * HALF, (half + 1) * HALF)
-            acc = banks.tile([P, HALF], F32, name=f"acc{half}", tag=("first_scores", "mid_scores")[half])
+        pieces = (
+            (slice(0, HALF), "first_scores", nc.scalar.copy, nc.scalar),
+            (slice(HALF, HALF + P), "mid_scores", nc.vector.tensor_copy, nc.sync),
+            (slice(HALF + P, E), "last_scores", nc.vector.tensor_copy, nc.sync),
+        )
+        for n, (cols, bank, engine_copy, queue) in enumerate(pieces):
+            width = cols.stop - cols.start
+            acc = banks.tile([P, width], F32, name=f"acc{n}", tag=bank)
             multiply(acc[:], w_codes[:], w_scales[:], v_codes[:, cols], v_scales[:, cols])
-            result = sbuf([P, HALF], F32, f"result{half}")
-            if half == 0:
-                nc.scalar.copy(result[:], acc[:])
-                nc.scalar.dma_start(out[:, cols], result[:])
-            else:
-                nc.vector.tensor_copy(result[:], acc[:])
-                nc.sync.dma_start(out[:, cols], result[:])
+            result = sbuf([P, width], F32, f"result{n}")
+            engine_copy(result[:], acc[:])
+            queue.dma_start(out[:, cols], result[:])

@@ -32,18 +32,17 @@ def tile_attend_sparq_kernel(tc, query, keys, size, vals, offs, out):
             return held.tile(shape, dtype, name=name, tag=after or name, align_bytes=64)
 
         offsets = held.tile([P, I // 16], U16, name="offsets")
+        nc.sync.dma_start(offsets[:], offs)
         q_raw = sbuf([P, D], F32, "q_raw")
         nc.sync.dma_start(q_raw[:], query)
-        nc.sync.dma_start(offsets[:], offs)
         k_raw = []
         for c in range(KEY_TILES):
             u, h = divmod(c, 2)
             raw = sbuf([P, D], F32, f"k_raw{c}")
             nc.sync.dma_start(raw[:], keys[256 * h + u : 256 * (h + 1) : 2, :])
             k_raw.append(raw)
-            if c == 0:
-                size_cols = sbuf([P, 2, 2], F32, "size_cols")
-                nc.sync.dma_start(size_cols[:], size[0, :].rearrange("(h r u) -> r h u", h=2, u=2))
+        size_cols = sbuf([P, PACK], F32, "size_cols")
+        nc.sync.dma_start(size_cols[:], size[0, :].rearrange("(r j) -> r j", j=PACK))
         v_raw = []
         for half in range(2):
             raw = sbuf([P, PACK, HALF], F32, f"v_raw{half}")
@@ -52,8 +51,6 @@ def tile_attend_sparq_kernel(tc, query, keys, size, vals, offs, out):
 
         ident = sbuf([P, P], F32, "ident")
         make_identity(nc, ident[:])
-        warm = sbuf([P, 1], F32, "warm")
-        nc.scalar.activation(warm[:], ident[:, 0:1], ACT.Exp)
 
         def quantize(codes, scales, grouped):
             nc.vector.quantize_mx(out=codes.bitcast(FP8X4), scales=scales, in_=grouped)
@@ -89,9 +86,9 @@ def tile_attend_sparq_kernel(tc, query, keys, size, vals, offs, out):
             return picked
 
         size_rows = banks.tile([P, T], F32, name="size_rows")
-        for c in range(KEY_TILES):
-            u, h = divmod(c, 2)
-            nc.tensor.transpose(size_rows[:, c * P : (c + 1) * P], size_cols[:, h, u : u + 1].to_broadcast([P, P]), ident[:])
+        for j in range(PACK):
+            nc.tensor.transpose(size_rows[:, j * P : (j + 1) * P], size_cols[:, j : j + 1].to_broadcast([P, P]), ident[:])
+        size_dealt = size_rows[:].rearrange("q (e u n) -> q u n e", e=2, u=2)
 
         first_grouped = sbuf([P, 2 * I], BF16, "first_grouped")
         mid_grouped = sbuf([P, 2 * I], BF16, "mid_grouped")
@@ -116,19 +113,16 @@ def tile_attend_sparq_kernel(tc, query, keys, size, vals, offs, out):
 
 
         q_codes, q_scales = first_codes[:, :P], first_scales[:, :P]
-        first_scores = banks.tile([P, P], F32, name="first_scores")
-        mid_scores = banks.tile([P, 2 * P], F32, name="mid_scores")
+        early_scores = banks.tile([P, 3 * P], F32, name="early_scores")
         last_scores = banks.tile([P, P], F32, name="last_scores")
-        multiply(first_scores[:], q_codes, q_scales, first_codes[:, P:], first_scales[:, P:])
-        multiply(mid_scores[:], q_codes, q_scales, mid_codes, mid_scales[:])
+        multiply(early_scores[:, :P], q_codes, q_scales, first_codes[:, P:], first_scales[:, P:])
+        multiply(early_scores[:, P:], q_codes, q_scales, mid_codes, mid_scales[:])
         multiply(last_scores[:], q_codes, q_scales, last_codes[:], last_scales[:])
 
         negated = sbuf([P, T], F32, "negated")
-        first_least = sbuf([P, 1], F32, "first_least")
         mid_least = sbuf([P, 1], F32, "mid_least")
         least = sbuf([P, 1], F32, "least")
-        nc.vector.tensor_scalar(negated[:, :P], first_scores[:], -1.0, None, ALU.mult, ALU.min, accum_out=first_least[:])
-        nc.vector.tensor_scalar(negated[:, P : 3 * P], mid_scores[:], -1.0, first_least[:], ALU.mult, ALU.min, accum_out=mid_least[:])
+        nc.vector.tensor_scalar(negated[:, : 3 * P], early_scores[:], -1.0, None, ALU.mult, ALU.min, accum_out=mid_least[:])
         nc.vector.tensor_scalar(negated[:, 3 * P :], last_scores[:], -1.0, mid_least[:], ALU.mult, ALU.min, accum_out=least[:])
 
 
@@ -155,7 +149,14 @@ def tile_attend_sparq_kernel(tc, query, keys, size, vals, offs, out):
         for u in range(2):
             cols = slice(u * (T // 2), (u + 1) * (T // 2))
             w = sbuf([P, T // 2], BF16, f"w{u}")
-            nc.vector.scalar_tensor_tensor(w[:], p[:, cols], p_inv[:], size_rows[:, cols], ALU.mult, ALU.mult)
+            nc.vector.scalar_tensor_tensor(
+                w[:].rearrange("q (n e) -> q n e", e=2),
+                p[:, cols].rearrange("q (n e) -> q n e", e=2),
+                p_inv[:],
+                size_dealt[:, u],
+                ALU.mult,
+                ALU.mult,
+            )
             nc.tensor.transpose(w_turned[:, u, :], w[:].bitcast(F32), ident[:])
         w_grouped = sbuf([P, T], BF16, "w_grouped")
         leave_psum(w_grouped[:], w_turned)
@@ -170,8 +171,8 @@ def tile_attend_sparq_kernel(tc, query, keys, size, vals, offs, out):
         w_scales = sbuf([P, P], U8, "w_scales")
         quantize(w_codes[:], w_scales[:], w_grouped[:])
         pieces = (
-            (slice(0, HALF), "first_scores", nc.scalar.copy, nc.scalar),
-            (slice(HALF, HALF + P), "mid_scores", nc.vector.tensor_copy, nc.sync),
+            (slice(0, HALF), "early_scores", nc.scalar.copy, nc.scalar),
+            (slice(HALF, HALF + P), "spare", nc.vector.tensor_copy, nc.sync),
             (slice(HALF + P, E), "last_scores", nc.vector.tensor_copy, nc.sync),
         )
         for n, (cols, bank, engine_copy, queue) in enumerate(pieces):

@@ -17,21 +17,23 @@ ACT = mybir.ActivationFunctionType
 
 P = 128
 PACK = 4
+RUN = 16
 KEY_TILES = T // P
-HALF = E // 2
+EARLY = (KEY_TILES - 1) * P
+TURN_BANKS = 3
 
 
 def tile_attend_sparq_kernel(tc, query, keys, size, vals, offs, out):
     nc = tc.nc
     with ExitStack() as ctx:
         held = ctx.enter_context(tc.tile_pool(name="held", bufs=1))
-        turn = ctx.enter_context(tc.psum_pool(name="turn", bufs=3))
+        turn = ctx.enter_context(tc.psum_pool(name="turn", bufs=TURN_BANKS))
         banks = ctx.enter_context(tc.psum_pool(name="banks", bufs=1))
 
         def sbuf(shape, dtype, name, after=None):
             return held.tile(shape, dtype, name=name, tag=after or name, align_bytes=64)
 
-        offsets = held.tile([P, I // 16], U16, name="offsets")
+        offsets = held.tile([P, I // RUN], U16, name="offsets")
         nc.sync.dma_start(offsets[:], offs)
         q_raw = sbuf([P, D], F32, "q_raw")
         nc.sync.dma_start(q_raw[:], query)
@@ -39,15 +41,12 @@ def tile_attend_sparq_kernel(tc, query, keys, size, vals, offs, out):
         for c in range(KEY_TILES):
             u, h = divmod(c, 2)
             raw = sbuf([P, D], F32, f"k_raw{c}")
-            nc.sync.dma_start(raw[:], keys[256 * h + u : 256 * (h + 1) : 2, :])
+            nc.sync.dma_start(raw[:], keys[2 * P * h + u : 2 * P * (h + 1) : 2, :])
             k_raw.append(raw)
         size_cols = sbuf([P, PACK], F32, "size_cols")
         nc.sync.dma_start(size_cols[:], size[0, :].rearrange("(r j) -> r j", j=PACK))
-        v_raw = []
-        for half in range(2):
-            raw = sbuf([P, PACK, HALF], F32, f"v_raw{half}")
-            nc.sync.dma_start(raw[:], vals[:, half * HALF : (half + 1) * HALF].rearrange("(p j) e -> p j e", j=PACK))
-            v_raw.append(raw)
+        v_raw = sbuf([P, PACK, E], F32, "v_raw")
+        nc.sync.dma_start(v_raw[:], vals.rearrange("(p j) e -> p j e", j=PACK))
 
         ident = sbuf([P, P], F32, "ident")
         make_identity(nc, ident[:])
@@ -75,15 +74,14 @@ def tile_attend_sparq_kernel(tc, query, keys, size, vals, offs, out):
         def scalar_gather(dest, listed):
             nc.scalar.activation(dest, listed, ACT.Copy)
 
-        def gather_and_turn(gather, raw, grouped, name):
+        def gather_and_turn(gather, window, grouped, name):
             picked = sbuf([P, I], BF16, f"{name}_picked")
-            gather(picked[:].rearrange("r (u g y) -> r g u y", u=2, y=16), raw[:].indirect(offsets[:]))
+            gather(picked[:].rearrange("r (u g y) -> r g u y", u=2, y=RUN), window[:].indirect(offsets[:]))
             words = picked[:].bitcast(F32)
             turned = turn.tile([P, 2, P], F32, name="turned")
             for u in range(2):
                 nc.tensor.transpose(turned[:, u, :], words[:, u * P : (u + 1) * P], ident[:])
             leave_psum(grouped, turned)
-            return picked
 
         size_rows = banks.tile([P, T], F32, name="size_rows")
         for j in range(PACK):
@@ -99,7 +97,7 @@ def tile_attend_sparq_kernel(tc, query, keys, size, vals, offs, out):
         gather_and_turn(scalar_gather, k0_rounded, first_grouped[:, I:], "k0")
         gather_and_turn(nc.vector.tensor_copy, k_raw[1], mid_grouped[:, :I], "k1")
         gather_and_turn(nc.vector.tensor_copy, k_raw[2], mid_grouped[:, I:], "k2")
-        last_picked = gather_and_turn(nc.vector.tensor_copy, k_raw[3], last_grouped[:], "k3")
+        gather_and_turn(nc.vector.tensor_copy, k_raw[3], last_grouped[:], "k3")
 
         early_codes = sbuf([P, 4 * P], U32, "early_codes", after="k_raw3")
         first_codes, mid_codes = early_codes[:, : 2 * P], early_codes[:, 2 * P :]
@@ -111,47 +109,44 @@ def tile_attend_sparq_kernel(tc, query, keys, size, vals, offs, out):
         quantize(mid_codes, mid_scales[:], mid_grouped[:])
         quantize(last_codes[:], last_scales[:], last_grouped[:])
 
-
         q_codes, q_scales = first_codes[:, :P], first_scales[:, :P]
-        early_scores = banks.tile([P, 3 * P], F32, name="early_scores")
+        early_scores = banks.tile([P, EARLY], F32, name="early_scores")
         last_scores = banks.tile([P, P], F32, name="last_scores")
         multiply(early_scores[:, :P], q_codes, q_scales, first_codes[:, P:], first_scales[:, P:])
         multiply(early_scores[:, P:], q_codes, q_scales, mid_codes, mid_scales[:])
         multiply(last_scores[:], q_codes, q_scales, last_codes[:], last_scales[:])
 
         negated = sbuf([P, T], F32, "negated")
-        mid_least = sbuf([P, 1], F32, "mid_least")
+        early_least = sbuf([P, 1], F32, "early_least")
         least = sbuf([P, 1], F32, "least")
-        nc.vector.tensor_scalar(negated[:, : 3 * P], early_scores[:], -1.0, None, ALU.mult, ALU.min, accum_out=mid_least[:])
-        nc.vector.tensor_scalar(negated[:, 3 * P :], last_scores[:], -1.0, mid_least[:], ALU.mult, ALU.min, accum_out=least[:])
+        nc.vector.tensor_scalar(negated[:, :EARLY], early_scores[:], -1.0, None, ALU.mult, ALU.min, accum_out=early_least[:])
+        nc.vector.tensor_scalar(negated[:, EARLY:], last_scores[:], -1.0, early_least[:], ALU.mult, ALU.min, accum_out=least[:])
 
-
-        def interleave(engine_copy, raw, cols, name, after):
-            width = cols.stop - cols.start
-            grouped = sbuf([P, width * PACK], BF16, name, after=after)
+        def interleave(engine_copy, cols, name, after):
+            grouped = sbuf([P, (cols.stop - cols.start) * PACK], BF16, name, after=after)
             engine_copy(
                 grouped[:].rearrange("p (c u e) -> p c u e", u=2, e=2),
-                raw[:, :, cols].rearrange("p (e u) c -> p c u e", u=2),
+                v_raw[:, :, cols].rearrange("p (e u) c -> p c u e", u=2),
             )
             return grouped
 
-        v_grouped0 = interleave(nc.scalar.copy, v_raw[0], slice(0, P), "v_grouped0", "k3_picked")
+        v_ahead, v_behind, v_during = slice(0, E // 4), slice(E // 4, E // 2), slice(E // 2, E)
+        ahead_grouped = interleave(nc.scalar.copy, v_ahead, "ahead_grouped", "k3_picked")
 
         p = sbuf([P, T], F32, "p")
         p_sum = sbuf([P, 1], F32, "p_sum")
         nc.scalar.activation(p[:], negated[:], ACT.Exp, bias=least[:], scale=-1.0, accum_out=p_sum[:])
-        v_grouped1 = interleave(nc.scalar.copy, v_raw[0], slice(P, HALF), "v_grouped1", "negated")
-        v_grouped2 = interleave(nc.vector.tensor_copy, v_raw[1], slice(0, HALF), "v_grouped2", "mid_least")
+        behind_grouped = interleave(nc.scalar.copy, v_behind, "behind_grouped", "negated")
+        during_grouped = interleave(nc.vector.tensor_copy, v_during, "during_grouped", "early_least")
         p_inv = sbuf([P, 1], F32, "p_inv")
         nc.vector.reciprocal(p_inv[:], p_sum[:])
 
         w_turned = turn.tile([P, 2, P], F32, name="turned")
         for u in range(2):
-            cols = slice(u * (T // 2), (u + 1) * (T // 2))
             w = sbuf([P, T // 2], BF16, f"w{u}")
             nc.vector.scalar_tensor_tensor(
                 w[:].rearrange("q (n e) -> q n e", e=2),
-                p[:, cols].rearrange("q (n e) -> q n e", e=2),
+                p[:, u * (T // 2) : (u + 1) * (T // 2)].rearrange("q (n e) -> q n e", e=2),
                 p_inv[:],
                 size_dealt[:, u],
                 ALU.mult,
@@ -163,17 +158,17 @@ def tile_attend_sparq_kernel(tc, query, keys, size, vals, offs, out):
 
         v_codes = sbuf([P, E], U32, "v_codes", after="p")
         v_scales = sbuf([P, E], U8, "v_scales")
-        quantize(v_codes[:, :P], v_scales[:, :P], v_grouped0[:])
-        quantize(v_codes[:, HALF:], v_scales[:, HALF:], v_grouped2[:])
-        quantize(v_codes[:, P:HALF], v_scales[:, P:HALF], v_grouped1[:])
+        for cols, grouped in ((v_ahead, ahead_grouped), (v_during, during_grouped), (v_behind, behind_grouped)):
+            quantize(v_codes[:, cols], v_scales[:, cols], grouped[:])
 
         w_codes = sbuf([P, P], U32, "w_codes")
         w_scales = sbuf([P, P], U8, "w_scales")
         quantize(w_codes[:], w_scales[:], w_grouped[:])
+
         pieces = (
-            (slice(0, HALF), "early_scores", nc.scalar.copy, nc.scalar),
-            (slice(HALF, HALF + P), "spare", nc.vector.tensor_copy, nc.sync),
-            (slice(HALF + P, E), "last_scores", nc.vector.tensor_copy, nc.sync),
+            (slice(0, E // 2), "early_scores", nc.scalar.copy, nc.scalar),
+            (slice(E // 2, 3 * E // 4), "third_quarter", nc.vector.tensor_copy, nc.sync),
+            (slice(3 * E // 4, E), "last_scores", nc.vector.tensor_copy, nc.sync),
         )
         for n, (cols, bank, engine_copy, queue) in enumerate(pieces):
             width = cols.stop - cols.start

from contextlib import ExitStack

import concourse.mybir as mybir
from concourse.masks import make_identity

D, I, T, Q, E = 1024, 512, 512, 128, 512
FLOPS = 2 * Q * T * I + 2 * Q * E * T

F32 = mybir.dt.float32
BF16 = mybir.dt.bfloat16
U32 = mybir.dt.uint32
U16 = mybir.dt.uint16
U8 = mybir.dt.uint8
FP8X4 = mybir.dt.float8_e4m3fn_x4
ALU = mybir.AluOpType
ACT = mybir.ActivationFunctionType

P = 128
PACK = 4
RUN = 16
KEY_TILES = T // P
EARLY = (KEY_TILES - 1) * P
TURN_BANKS = 3


def tile_attend_sparq_kernel(tc, query, keys, size, vals, offs, out):
    nc = tc.nc
    with ExitStack() as ctx:
        held = ctx.enter_context(tc.tile_pool(name="held", bufs=1))
        turn = ctx.enter_context(tc.psum_pool(name="turn", bufs=TURN_BANKS))
        banks = ctx.enter_context(tc.psum_pool(name="banks", bufs=1))

        def sbuf(shape, dtype, name, after=None):
            return held.tile(shape, dtype, name=name, tag=after or name, align_bytes=64)

        offsets = held.tile([P, I // RUN], U16, name="offsets")
        nc.sync.dma_start(offsets[:], offs)
        q_raw = sbuf([P, D], F32, "q_raw")
        nc.sync.dma_start(q_raw[:], query)
        k_raw = []
        for c in range(KEY_TILES):
            u, h = divmod(c, 2)
            raw = sbuf([P, D], F32, f"k_raw{c}")
            nc.sync.dma_start(raw[:], keys[2 * P * h + u : 2 * P * (h + 1) : 2, :])
            k_raw.append(raw)
        size_cols = sbuf([P, PACK], F32, "size_cols")
        nc.sync.dma_start(size_cols[:], size[0, :].rearrange("(r j) -> r j", j=PACK))
        v_raw = sbuf([P, PACK, E], F32, "v_raw")
        nc.sync.dma_start(v_raw[:], vals.rearrange("(p j) e -> p j e", j=PACK))

        ident = sbuf([P, P], F32, "ident")
        make_identity(nc, ident[:])

        def quantize(codes, scales, grouped):
            nc.vector.quantize_mx(out=codes.bitcast(FP8X4), scales=scales, in_=grouped)

        def multiply(dest, lhs_codes, lhs_scales, rhs_codes, rhs_scales):
            nc.tensor.matmul_mx(
                out=dest,
                lhsT=lhs_codes.bitcast(FP8X4),
                lhsT_scale=lhs_scales,
                rhs=rhs_codes.bitcast(FP8X4),
                rhs_scale=rhs_scales,
                start=True,
                stop=True,
            )

        def leave_psum(grouped, turned):
            nc.scalar.copy(
                grouped.bitcast(F32).rearrange("p (r u) -> p r u", u=2),
                turned[:].rearrange("p u r -> p r u"),
            )

        def scalar_gather(dest, listed):
            nc.scalar.activation(dest, listed, ACT.Copy)

        def gather_and_turn(gather, window, grouped, name):
            picked = sbuf([P, I], BF16, f"{name}_picked")
            gather(picked[:].rearrange("r (u g y) -> r g u y", u=2, y=RUN), window[:].indirect(offsets[:]))
            words = picked[:].bitcast(F32)
            turned = turn.tile([P, 2, P], F32, name="turned")
            for u in range(2):
                nc.tensor.transpose(turned[:, u, :], words[:, u * P : (u + 1) * P], ident[:])
            leave_psum(grouped, turned)

        size_rows = banks.tile([P, T], F32, name="size_rows")
        for j in range(PACK):
            nc.tensor.transpose(size_rows[:, j * P : (j + 1) * P], size_cols[:, j : j + 1].to_broadcast([P, P]), ident[:])
        size_dealt = size_rows[:].rearrange("q (e u n) -> q u n e", e=2, u=2)

        first_grouped = sbuf([P, 2 * I], BF16, "first_grouped")
        mid_grouped = sbuf([P, 2 * I], BF16, "mid_grouped")
        last_grouped = sbuf([P, I], BF16, "last_grouped")
        gather_and_turn(nc.vector.tensor_copy, q_raw, first_grouped[:, :I], "q")
        k0_rounded = sbuf([P, D], BF16, "k0_rounded")
        nc.vector.tensor_copy(k0_rounded[:], k_raw[0][:])
        gather_and_turn(scalar_gather, k0_rounded, first_grouped[:, I:], "k0")
        gather_and_turn(nc.vector.tensor_copy, k_raw[1], mid_grouped[:, :I], "k1")
        gather_and_turn(nc.vector.tensor_copy, k_raw[2], mid_grouped[:, I:], "k2")
        gather_and_turn(nc.vector.tensor_copy, k_raw[3], last_grouped[:], "k3")

        early_codes = sbuf([P, 4 * P], U32, "early_codes", after="k_raw3")
        first_codes, mid_codes = early_codes[:, : 2 * P], early_codes[:, 2 * P :]
        first_scales = sbuf([P, 2 * P], U8, "first_scales")
        mid_scales = sbuf([P, 2 * P], U8, "mid_scales")
        last_codes = sbuf([P, P], U32, "last_codes")
        last_scales = sbuf([P, P], U8, "last_scales")
        quantize(first_codes, first_scales[:], first_grouped[:])
        quantize(mid_codes, mid_scales[:], mid_grouped[:])
        quantize(last_codes[:], last_scales[:], last_grouped[:])

        q_codes, q_scales = first_codes[:, :P], first_scales[:, :P]
        early_scores = banks.tile([P, EARLY], F32, name="early_scores")
        last_scores = banks.tile([P, P], F32, name="last_scores")
        multiply(early_scores[:, :P], q_codes, q_scales, first_codes[:, P:], first_scales[:, P:])
        multiply(early_scores[:, P:], q_codes, q_scales, mid_codes, mid_scales[:])
        multiply(last_scores[:], q_codes, q_scales, last_codes[:], last_scales[:])

        negated = sbuf([P, T], F32, "negated")
        early_least = sbuf([P, 1], F32, "early_least")
        least = sbuf([P, 1], F32, "least")
        nc.vector.tensor_scalar(negated[:, :EARLY], early_scores[:], -1.0, None, ALU.mult, ALU.min, accum_out=early_least[:])
        nc.vector.tensor_scalar(negated[:, EARLY:], last_scores[:], -1.0, early_least[:], ALU.mult, ALU.min, accum_out=least[:])

        def interleave(engine_copy, cols, name, after):
            grouped = sbuf([P, (cols.stop - cols.start) * PACK], BF16, name, after=after)
            engine_copy(
                grouped[:].rearrange("p (c u e) -> p c u e", u=2, e=2),
                v_raw[:, :, cols].rearrange("p (e u) c -> p c u e", u=2),
            )
            return grouped

        v_ahead, v_behind, v_during = slice(0, E // 4), slice(E // 4, E // 2), slice(E // 2, E)
        ahead_grouped = interleave(nc.scalar.copy, v_ahead, "ahead_grouped", "k3_picked")

        p = sbuf([P, T], F32, "p")
        p_sum = sbuf([P, 1], F32, "p_sum")
        nc.scalar.activation(p[:], negated[:], ACT.Exp, bias=least[:], scale=-1.0, accum_out=p_sum[:])
        behind_grouped = interleave(nc.scalar.copy, v_behind, "behind_grouped", "negated")
        during_grouped = interleave(nc.vector.tensor_copy, v_during, "during_grouped", "early_least")
        p_inv = sbuf([P, 1], F32, "p_inv")
        nc.vector.reciprocal(p_inv[:], p_sum[:])

        w_turned = turn.tile([P, 2, P], F32, name="turned")
        for u in range(2):
            w = sbuf([P, T // 2], BF16, f"w{u}")
            nc.vector.scalar_tensor_tensor(
                w[:].rearrange("q (n e) -> q n e", e=2),
                p[:, u * (T // 2) : (u + 1) * (T // 2)].rearrange("q (n e) -> q n e", e=2),
                p_inv[:],
                size_dealt[:, u],
                ALU.mult,
                ALU.mult,
            )
            nc.tensor.transpose(w_turned[:, u, :], w[:].bitcast(F32), ident[:])
        w_grouped = sbuf([P, T], BF16, "w_grouped")
        leave_psum(w_grouped[:], w_turned)

        v_codes = sbuf([P, E], U32, "v_codes", after="p")
        v_scales = sbuf([P, E], U8, "v_scales")
        for cols, grouped in ((v_ahead, ahead_grouped), (v_during, during_grouped), (v_behind, behind_grouped)):
            quantize(v_codes[:, cols], v_scales[:, cols], grouped[:])

        w_codes = sbuf([P, P], U32, "w_codes")
        w_scales = sbuf([P, P], U8, "w_scales")
        quantize(w_codes[:], w_scales[:], w_grouped[:])

        pieces = (
            (slice(0, E // 2), "early_scores", nc.scalar.copy, nc.scalar),
            (slice(E // 2, 3 * E // 4), "third_quarter", nc.vector.tensor_copy, nc.sync),
            (slice(3 * E // 4, E), "last_scores", nc.vector.tensor_copy, nc.sync),
        )
        for n, (cols, bank, engine_copy, queue) in enumerate(pieces):
            width = cols.stop - cols.start
            acc = banks.tile([P, width], F32, name=f"acc{n}", tag=bank)
            multiply(acc[:], w_codes[:], w_scales[:], v_codes[:, cols], v_scales[:, cols])
            result = sbuf([P, width], F32, f"result{n}")
            engine_copy(result[:], acc[:])
            queue.dma_start(out[:, cols], result[:])
